import numpy as np
import ml_dtypes


def mxq(x, axis, fmt="e4m3"):
    dtype, down = {"e4m3": (ml_dtypes.float8_e4m3fn, 7), "e5m2": (ml_dtypes.float8_e5m2, 14)}[fmt]
    v = np.moveaxis(np.asarray(x, np.float32).astype(ml_dtypes.bfloat16).astype(np.float64), axis, -1)
    blocks = v.reshape(v.shape[:-1] + (-1, 32))
    amax = np.abs(blocks).max(-1, keepdims=True)
    byte = np.maximum(np.where(amax > 0, np.frexp(amax)[1] - 1 + 127, 0) - down, 1)
    scale = np.exp2(byte - 127.0)
    codes = (blocks / scale).astype(np.float32).astype(dtype).astype(np.float64)
    return np.moveaxis((codes * scale).reshape(v.shape), -1, axis)


WIDE = False


def mx_kscale(k):
    if not WIDE:
        return np.ones(k)
    levels = np.array([10, -10, 5, -5, 0])
    if k % 512:
        return np.exp2(np.random.permutation(np.resize(levels, k // 32))).repeat(32)
    a = np.empty((k // 512, 16))
    for p in range(k // 512):
        a[p, :8] = np.random.permutation(np.resize(levels, 8))
        for g in range(8):
            far = levels[np.abs(levels - a[p, g]) >= 10]
            a[p, g + 8] = far[np.random.randint(len(far))]
    return np.exp2(a.ravel()).repeat(32)


def f64(x):
    return np.asarray(x).astype(np.float64)


def striped(idx):
    return np.tile(idx.reshape(-1, 16).T, (8, 1)).astype(np.uint16)


def unstriped(offs):
    return offs[:16].T.reshape(-1).astype(np.int64)


def silu(v):
    return v / (1.0 + np.exp(-np.maximum(v, -700.0)))


K, T, S, N = 1024, 256, 768, 2048


def setup_inputs():
    n = np.random.standard_normal
    s = mx_kscale(K)[:, None]
    return {
        "w": (n((K, N)) / np.sqrt(K) / s).astype(np.float32),
        "xT": (n((K, T)) * s).astype(np.float32),
        "b": (0.3 * n((S, 1))).astype(np.float32),
        "offs": striped(np.sort(np.random.permutation(N)[:S])),
    }


def reference(w, xT, b, offs):
    idx = unstriped(offs)
    wq = mxq(f64(w)[:, idx], 0, "e4m3")
    return silu((wq.T @ mxq(f64(xT), 0, "e4m3")) + f64(b))

@@ -1,0 +1,129 @@
+from contextlib import ExitStack
+
+import concourse.mybir as mybir
+from concourse.masks import make_identity
+
+K, T, S, N = 1024, 256, 768, 2048
+FLOPS = 2 * K * T * S
+
+F32 = mybir.dt.float32
+BF16 = mybir.dt.bfloat16
+U32 = mybir.dt.uint32
+U16 = mybir.dt.uint16
+U8 = mybir.dt.uint8
+FP8X4 = mybir.dt.float8_e4m3fn_x4
+SILU = mybir.ActivationFunctionType.Silu
+
+P = 128
+ROWS = 4
+PASSES = K // (P * ROWS)
+BLOCK = 128
+BLOCKS = S // BLOCK
+SLICE = 256
+SLICES = S // SLICE
+
+
+def tile_picked_neuron_lin_silu_srt_e_kernel(tc, w, xT, b, offs, out):
+    nc = tc.nc
+    with ExitStack() as ctx:
+        keep = ctx.enter_context(tc.tile_pool(name="keep", bufs=1))
+        psum = ctx.enter_context(tc.psum_pool(name="psum", bufs=1))
+
+        offsets = keep.tile([P, S // 16], U16, name="offsets")
+        w_rows = [[keep.tile([P, N], F32, name=f"w{a}{j}") for j in range(ROWS)] for a in range(PASSES)]
+        x_rows = [keep.tile([P, ROWS, T], F32, name=f"x{a}") for a in range(PASSES)]
+
+        b_rows = keep.tile([P, P], F32, name="b_rows")
+        nc.vector.memset(b_rows[:], 0.0)
+        nc.scalar.dma_start(b_rows[0:BLOCKS, :], b.rearrange("(c p) o -> c (p o)", p=P))
+
+        warm = keep.tile([P, 2], F32, name="warm")
+        nc.vector.memset(warm[:, 0:1], 0.0)
+        nc.scalar.activation(warm[:, 1:2], warm[:, 0:1], SILU)
+
+        w_view = w.rearrange("(a p j) n -> a p j n", a=PASSES, j=ROWS)
+        x_view = xT.rearrange("(a p j) t -> a p j t", a=PASSES, j=ROWS)
+        nc.sync.dma_start(offsets[:], offs)
+        windows = [N] * SLICES
+        for a in range(PASSES):
+            for j in range(ROWS):
+                if (a, j) == (PASSES - 1, ROWS - 1):
+                    windows = [N - S + (s + 1) * SLICE for s in range(SLICES)]
+                    start = 0
+                    for stop in windows:
+                        nc.sync.dma_start(w_rows[a][j][:, start:stop], w_view[a, :, j, start:stop])
+                        start = stop
+                else:
+                    nc.sync.dma_start(w_rows[a][j][:], w_view[a, :, j, :])
+                    if a == 0 and j in (1, 3):
+                        nc.sync.dma_start(x_rows[j // 2][:], x_view[j // 2])
+
+        x_codes, x_scales = [], []
+        for a in range(PASSES):
+            grouped = keep.tile([P, T, ROWS], BF16, name=f"xg{a}", align_bytes=64)
+            nc.scalar.copy(grouped[:], x_rows[a][:].rearrange("p j t -> p t j"))
+            codes = keep.tile([P, T], U32, name=f"xc{a}", align_bytes=64)
+            scales = keep.tile([P, T], U8, name=f"xs{a}", align_bytes=64)
+            nc.vector.quantize_mx(
+                out=codes[:].bitcast(FP8X4), scales=scales[:], in_=grouped[:].rearrange("p t j -> p (t j)")
+            )
+            x_codes.append(codes)
+            x_scales.append(scales)
+
+        sums = [psum.tile([P, T], F32, name=f"sums{c}") for c in range(BLOCKS)]
+        for a in range(PASSES):
+            last = a == PASSES - 1
+            if last:
+                identity = keep.tile([P, P], F32, name="identity")
+                bias = keep.tile([P, BLOCKS], F32, name="bias")
+                make_identity(nc, identity[:])
+                b_turned = psum.tile([P, P], F32, name="b_turned")
+                nc.tensor.transpose(b_turned[:], b_rows[:], identity[:])
+                nc.scalar.copy(bias[:], b_turned[:, 0:BLOCKS])
+            picked = keep.tile([P, ROWS, S], F32, name=f"picked{a}")
+            groups = [keep.tile([P, SLICE, ROWS], BF16, name=f"wg{a}{s}", align_bytes=64) for s in range(SLICES)]
+            for j in range(ROWS):
+                if last and j == ROWS - 1:
+                    for s in range(SLICES):
+                        e0, e1 = s * SLICE, (s + 1) * SLICE
+                        nc.vector.tensor_copy(
+                            picked[:, j, e0:e1],
+                            w_rows[a][j][:, 0 : windows[s]].indirect(offsets[:, e0 // 16 : e1 // 16]),
+                        )
+                else:
+                    nc.vector.tensor_copy(picked[:, j, :], w_rows[a][j][:].indirect(offsets[:]))
+                if last and j == 1:
+                    for s in range(SLICES):
+                        nc.scalar.copy(
+                            groups[s][:, :, 0:2],
+                            picked[:, 0:2, s * SLICE : (s + 1) * SLICE].rearrange("p j n -> p n j"),
+                        )
+            for s in range(SLICES):
+                e = slice(s * SLICE, (s + 1) * SLICE)
+                if not last:
+                    nc.scalar.copy(groups[s][:], picked[:, :, e].rearrange("p j n -> p n j"))
+                elif s == SLICES - 1:
+                    nc.vector.tensor_copy(groups[s][:, :, 2:4], picked[:, 2:4, e].rearrange("p j n -> p n j"))
+                else:
+                    nc.scalar.copy(groups[s][:, :, 2:4], picked[:, 2:4, e].rearrange("p j n -> p n j"))
+                codes = keep.tile([P, SLICE], U32, name=f"wc{a}{s}", align_bytes=64)
+                scales = keep.tile([P, SLICE], U8, name=f"ws{a}{s}", align_bytes=64)
+                nc.vector.quantize_mx(
+                    out=codes[:].bitcast(FP8X4), scales=scales[:], in_=groups[s][:].rearrange("p n j -> p (n j)")
+                )
+                for h in range(SLICE // BLOCK):
+                    c = s * (SLICE // BLOCK) + h
+                    m = slice(h * BLOCK, (h + 1) * BLOCK)
+                    nc.tensor.matmul_mx(
+                        out=sums[c][:],
+                        lhsT=codes[:, m].bitcast(FP8X4),
+                        lhsT_scale=scales[:, m],
+                        rhs=x_codes[a][:].bitcast(FP8X4),
+                        rhs_scale=x_scales[a][:],
+                        start=(a == 0),
+                        stop=last,
+                    )
+                    if last:
+                        result = keep.tile([P, T], F32, name=f"result{c}")
+                        nc.scalar.activation(result[:], sums[c][:], SILU, bias=bias[:, c : c + 1])
+                        nc.sync.dma_start(out[c * BLOCK : (c + 1) * BLOCK, :], result[:])

@@ -34,8 +34,7 @@ def tile_picked_neuron_lin_silu_srt_e_kernel(tc, w, xT, b, offs, out):
         x_rows = [keep.tile([P, ROWS, T], F32, name=f"x{a}") for a in range(PASSES)]
 
         b_rows = keep.tile([P, P], F32, name="b_rows")
-        nc.vector.memset(b_rows[:], 0.0)
-        nc.scalar.dma_start(b_rows[0:BLOCKS, :], b.rearrange("(c p) o -> c (p o)", p=P))
+        nc.gpsimd.memset(b_rows[:], 0.0)
 
         warm = keep.tile([P, 2], F32, name="warm")
         nc.vector.memset(warm[:, 0:1], 0.0)
@@ -43,87 +42,120 @@ def tile_picked_neuron_lin_silu_srt_e_kernel(tc, w, xT, b, offs, out):
 
         w_view = w.rearrange("(a p j) n -> a p j n", a=PASSES, j=ROWS)
         x_view = xT.rearrange("(a p j) t -> a p j t", a=PASSES, j=ROWS)
+        nc.sync.dma_start(x_rows[0][:], x_view[0])
         nc.sync.dma_start(offsets[:], offs)
-        windows = [N] * SLICES
-        for a in range(PASSES):
-            for j in range(ROWS):
-                if (a, j) == (PASSES - 1, ROWS - 1):
-                    windows = [N - S + (s + 1) * SLICE for s in range(SLICES)]
-                    start = 0
-                    for stop in windows:
-                        nc.sync.dma_start(w_rows[a][j][:, start:stop], w_view[a, :, j, start:stop])
-                        start = stop
-                else:
-                    nc.sync.dma_start(w_rows[a][j][:], w_view[a, :, j, :])
-                    if a == 0 and j in (1, 3):
-                        nc.sync.dma_start(x_rows[j // 2][:], x_view[j // 2])
-
-        x_codes, x_scales = [], []
-        for a in range(PASSES):
+        nc.sync.dma_start(b_rows[0:BLOCKS, :], b.rearrange("(c p) o -> c (p o)", p=P))
+        nc.sync.dma_start(x_rows[1][:], x_view[1])
+        nc.sync.dma_start(w_rows[0][0][:], w_view[0, :, 0, :])
+        nc.sync.dma_start(w_rows[0][1][:], w_view[0, :, 1, :])
+        nc.sync.dma_start(w_rows[0][2][:], w_view[0, :, 2, :])
+        nc.sync.dma_start(w_rows[0][3][:], w_view[0, :, 3, :])
+        nc.sync.dma_start(w_rows[1][0][:], w_view[1, :, 0, :])
+        nc.sync.dma_start(w_rows[1][1][:], w_view[1, :, 1, :])
+        nc.sync.dma_start(w_rows[1][2][:], w_view[1, :, 2, :])
+        nc.sync.dma_start(w_rows[1][3][:], w_view[1, :, 3, :])
+        x_codes, x_scales = [None, None], [None, None]
+        sums = [psum.tile([P, T], F32, name=f"sums{c}") for c in range(BLOCKS)]
+        picked = [keep.tile([P, ROWS, S], F32, name=f"picked{a}") for a in range(PASSES)]
+        slices = [(0, 256), (256, 512), (512, 768)]
+        groups = [[keep.tile([P, s1 - s0, ROWS], BF16, name=f"wg{a}{s0}", align_bytes=64) for (s0, s1) in slices] for a in range(PASSES)]
+        def do_x(a, eng):
             grouped = keep.tile([P, T, ROWS], BF16, name=f"xg{a}", align_bytes=64)
-            nc.scalar.copy(grouped[:], x_rows[a][:].rearrange("p j t -> p t j"))
+            eng(grouped[:], x_rows[a][:].rearrange("p j t -> p t j"))
             codes = keep.tile([P, T], U32, name=f"xc{a}", align_bytes=64)
             scales = keep.tile([P, T], U8, name=f"xs{a}", align_bytes=64)
             nc.vector.quantize_mx(
                 out=codes[:].bitcast(FP8X4), scales=scales[:], in_=grouped[:].rearrange("p t j -> p (t j)")
             )
-            x_codes.append(codes)
-            x_scales.append(scales)
+            x_codes[a], x_scales[a] = codes, scales
 
-        sums = [psum.tile([P, T], F32, name=f"sums{c}") for c in range(BLOCKS)]
-        for a in range(PASSES):
-            last = a == PASSES - 1
-            if last:
-                identity = keep.tile([P, P], F32, name="identity")
-                bias = keep.tile([P, BLOCKS], F32, name="bias")
-                make_identity(nc, identity[:])
-                b_turned = psum.tile([P, P], F32, name="b_turned")
-                nc.tensor.transpose(b_turned[:], b_rows[:], identity[:])
-                nc.scalar.copy(bias[:], b_turned[:, 0:BLOCKS])
-            picked = keep.tile([P, ROWS, S], F32, name=f"picked{a}")
-            groups = [keep.tile([P, SLICE, ROWS], BF16, name=f"wg{a}{s}", align_bytes=64) for s in range(SLICES)]
-            for j in range(ROWS):
-                if last and j == ROWS - 1:
-                    for s in range(SLICES):
-                        e0, e1 = s * SLICE, (s + 1) * SLICE
-                        nc.vector.tensor_copy(
-                            picked[:, j, e0:e1],
-                            w_rows[a][j][:, 0 : windows[s]].indirect(offsets[:, e0 // 16 : e1 // 16]),
-                        )
-                else:
-                    nc.vector.tensor_copy(picked[:, j, :], w_rows[a][j][:].indirect(offsets[:]))
-                if last and j == 1:
-                    for s in range(SLICES):
-                        nc.scalar.copy(
-                            groups[s][:, :, 0:2],
-                            picked[:, 0:2, s * SLICE : (s + 1) * SLICE].rearrange("p j n -> p n j"),
-                        )
-            for s in range(SLICES):
-                e = slice(s * SLICE, (s + 1) * SLICE)
-                if not last:
-                    nc.scalar.copy(groups[s][:], picked[:, :, e].rearrange("p j n -> p n j"))
-                elif s == SLICES - 1:
-                    nc.vector.tensor_copy(groups[s][:, :, 2:4], picked[:, 2:4, e].rearrange("p j n -> p n j"))
-                else:
-                    nc.scalar.copy(groups[s][:, :, 2:4], picked[:, 2:4, e].rearrange("p j n -> p n j"))
-                codes = keep.tile([P, SLICE], U32, name=f"wc{a}{s}", align_bytes=64)
-                scales = keep.tile([P, SLICE], U8, name=f"ws{a}{s}", align_bytes=64)
-                nc.vector.quantize_mx(
-                    out=codes[:].bitcast(FP8X4), scales=scales[:], in_=groups[s][:].rearrange("p n j -> p (n j)")
+        def gather(a, j, e0, e1, window):
+            nc.vector.tensor_copy(
+                picked[a][:, j, e0:e1], w_rows[a][j][:, 0:window].indirect(offsets[:, e0 // 16 : e1 // 16])
+            )
+
+        def weave(a, s, j0, j1, eng):
+            e0, e1 = slices[s]
+            eng(groups[a][s][:, :, j0:j1], picked[a][:, j0:j1, e0:e1].rearrange("p j n -> p n j"))
+
+        def finish(a, s):
+            e0, e1 = slices[s]
+            codes = keep.tile([P, e1 - e0], U32, name=f"wc{a}{e0}", align_bytes=64)
+            scales = keep.tile([P, e1 - e0], U8, name=f"ws{a}{e0}", align_bytes=64)
+            nc.vector.quantize_mx(
+                out=codes[:].bitcast(FP8X4), scales=scales[:], in_=groups[a][s][:].rearrange("p n j -> p (n j)")
+            )
+            return codes, scales
+
+        def multiply(a, s, codes, scales):
+            e0, e1 = slices[s]
+            for h in range((e1 - e0) // BLOCK):
+                c = e0 // BLOCK + h
+                m = slice(h * BLOCK, (h + 1) * BLOCK)
+                nc.tensor.matmul_mx(
+                    out=sums[c][:],
+                    lhsT=codes[:, m].bitcast(FP8X4),
+                    lhsT_scale=scales[:, m],
+                    rhs=x_codes[a][:].bitcast(FP8X4),
+                    rhs_scale=x_scales[a][:],
+                    start=(a == 0),
+                    stop=(a == 1),
                 )
-                for h in range(SLICE // BLOCK):
-                    c = s * (SLICE // BLOCK) + h
-                    m = slice(h * BLOCK, (h + 1) * BLOCK)
-                    nc.tensor.matmul_mx(
-                        out=sums[c][:],
-                        lhsT=codes[:, m].bitcast(FP8X4),
-                        lhsT_scale=scales[:, m],
-                        rhs=x_codes[a][:].bitcast(FP8X4),
-                        rhs_scale=x_scales[a][:],
-                        start=(a == 0),
-                        stop=last,
-                    )
-                    if last:
-                        result = keep.tile([P, T], F32, name=f"result{c}")
-                        nc.scalar.activation(result[:], sums[c][:], SILU, bias=bias[:, c : c + 1])
-                        nc.sync.dma_start(out[c * BLOCK : (c + 1) * BLOCK, :], result[:])
+
+        def emit(s):
+            e0, e1 = slices[s]
+            for c in range(e0 // BLOCK, e1 // BLOCK):
+                result = keep.tile([P, T], F32, name=f"result{c}")
+                nc.scalar.activation(result[:], sums[c][:], SILU, bias=bias[:, c : c + 1])
+                nc.sync.dma_start(out[c * BLOCK : (c + 1) * BLOCK, :], result[:])
+
+        def turn_bias():
+            identity = keep.tile([P, P], F32, name="identity")
+            bias = keep.tile([P, BLOCKS], F32, name="bias")
+            make_identity(nc, identity[:])
+            b_turned = psum.tile([P, P], F32, name="b_turned")
+            nc.tensor.transpose(b_turned[:], b_rows[:], identity[:])
+            nc.scalar.copy(bias[:], b_turned[:, 0:BLOCKS])
+            return bias
+
+        V, Sc, G = nc.vector.tensor_copy, nc.scalar.copy, nc.gpsimd.tensor_copy
+        do_x(0, V)
+        do_x(1, V)
+        gather(0, 0, 0, S, N)
+        gather(0, 1, 0, S, N)
+        bias = turn_bias()
+        weave(0, 0, 0, 2, Sc)
+        weave(0, 1, 0, 2, Sc)
+        weave(0, 2, 0, 2, Sc)
+        gather(0, 2, 0, S, N)
+        gather(0, 3, 0, S, N)
+        weave(0, 1, 2, 4, Sc)
+        weave(0, 0, 2, 4, V)
+        weave(0, 2, 2, 4, V)
+        q00 = finish(0, 0)
+        q01 = finish(0, 1)
+        q02 = finish(0, 2)
+        multiply(0, 0, *q00)
+        multiply(0, 1, *q01)
+        multiply(0, 2, *q02)
+        gather(1, 0, 0, S, N)
+        gather(1, 1, 0, S, N)
+        weave(1, 0, 0, 2, Sc)
+        weave(1, 1, 0, 2, Sc)
+        weave(1, 2, 0, 2, Sc)
+        gather(1, 2, 0, S, N)
+        gather(1, 3, 0, 256, N)
+        weave(1, 0, 2, 4, Sc)
+        gather(1, 3, 256, 512, N)
+        weave(1, 1, 2, 4, Sc)
+        q10 = finish(1, 0)
+        multiply(1, 0, *q10)
+        emit(0)
+        gather(1, 3, 512, 768, N)
+        q11 = finish(1, 1)
+        multiply(1, 1, *q11)
+        emit(1)
+        weave(1, 2, 2, 4, V)
+        q12 = finish(1, 2)
+        multiply(1, 2, *q12)
+        emit(2)

@@ -44,20 +44,21 @@ def tile_picked_neuron_lin_silu_srt_e_kernel(tc, w, xT, b, offs, out):
         x_view = xT.rearrange("(a p j) t -> a p j t", a=PASSES, j=ROWS)
         nc.sync.dma_start(x_rows[0][:], x_view[0])
         nc.sync.dma_start(offsets[:], offs)
-        nc.sync.dma_start(b_rows[0:BLOCKS, :], b.rearrange("(c p) o -> c (p o)", p=P))
-        nc.sync.dma_start(x_rows[1][:], x_view[1])
         nc.sync.dma_start(w_rows[0][0][:], w_view[0, :, 0, :])
+        nc.sync.dma_start(b_rows[0:BLOCKS, :], b.rearrange("(c p) o -> c (p o)", p=P))
         nc.sync.dma_start(w_rows[0][1][:], w_view[0, :, 1, :])
         nc.sync.dma_start(w_rows[0][2][:], w_view[0, :, 2, :])
         nc.sync.dma_start(w_rows[0][3][:], w_view[0, :, 3, :])
+        nc.sync.dma_start(x_rows[1][:], x_view[1])
         nc.sync.dma_start(w_rows[1][0][:], w_view[1, :, 0, :])
         nc.sync.dma_start(w_rows[1][1][:], w_view[1, :, 1, :])
         nc.sync.dma_start(w_rows[1][2][:], w_view[1, :, 2, :])
-        nc.sync.dma_start(w_rows[1][3][:], w_view[1, :, 3, :])
+        nc.sync.dma_start(w_rows[1][3][:, 0:1792], w_view[1, :, 3, 0:1792])
+        nc.sync.dma_start(w_rows[1][3][:, 1792:2048], w_view[1, :, 3, 1792:2048])
         x_codes, x_scales = [None, None], [None, None]
         sums = [psum.tile([P, T], F32, name=f"sums{c}") for c in range(BLOCKS)]
         picked = [keep.tile([P, ROWS, S], F32, name=f"picked{a}") for a in range(PASSES)]
-        slices = [(0, 256), (256, 512), (512, 768)]
+        slices = [[0, 256], [256, 512], [512, 640], [640, 768]]
         groups = [[keep.tile([P, s1 - s0, ROWS], BF16, name=f"wg{a}{s0}", align_bytes=64) for (s0, s1) in slices] for a in range(PASSES)]
         def do_x(a, eng):
             grouped = keep.tile([P, T, ROWS], BF16, name=f"xg{a}", align_bytes=64)
@@ -120,42 +121,51 @@ def tile_picked_neuron_lin_silu_srt_e_kernel(tc, w, xT, b, offs, out):
 
         V, Sc, G = nc.vector.tensor_copy, nc.scalar.copy, nc.gpsimd.tensor_copy
         do_x(0, V)
-        do_x(1, V)
         gather(0, 0, 0, S, N)
         gather(0, 1, 0, S, N)
         bias = turn_bias()
         weave(0, 0, 0, 2, Sc)
         weave(0, 1, 0, 2, Sc)
         weave(0, 2, 0, 2, Sc)
+        weave(0, 3, 0, 2, Sc)
         gather(0, 2, 0, S, N)
         gather(0, 3, 0, S, N)
         weave(0, 1, 2, 4, Sc)
         weave(0, 0, 2, 4, V)
         weave(0, 2, 2, 4, V)
+        weave(0, 3, 2, 4, Sc)
         q00 = finish(0, 0)
-        q01 = finish(0, 1)
         q02 = finish(0, 2)
+        q01 = finish(0, 1)
+        q03 = finish(0, 3)
         multiply(0, 0, *q00)
-        multiply(0, 1, *q01)
         multiply(0, 2, *q02)
+        multiply(0, 1, *q01)
+        multiply(0, 3, *q03)
+        do_x(1, Sc)
         gather(1, 0, 0, S, N)
         gather(1, 1, 0, S, N)
         weave(1, 0, 0, 2, Sc)
         weave(1, 1, 0, 2, Sc)
         weave(1, 2, 0, 2, Sc)
+        weave(1, 3, 0, 2, Sc)
         gather(1, 2, 0, S, N)
-        gather(1, 3, 0, 256, N)
+        gather(1, 3, 0, 256, 1792)
         weave(1, 0, 2, 4, Sc)
-        gather(1, 3, 256, 512, N)
+        gather(1, 3, 256, 512, 1792)
         weave(1, 1, 2, 4, Sc)
         q10 = finish(1, 0)
         multiply(1, 0, *q10)
         emit(0)
         gather(1, 3, 512, 768, N)
+        weave(1, 2, 2, 4, V)
         q11 = finish(1, 1)
         multiply(1, 1, *q11)
         emit(1)
-        weave(1, 2, 2, 4, V)
+        weave(1, 3, 2, 4, V)
         q12 = finish(1, 2)
         multiply(1, 2, *q12)
         emit(2)
+        q13 = finish(1, 3)
+        multiply(1, 3, *q13)
+        emit(3)

@@ -53,13 +53,14 @@ def tile_picked_neuron_lin_silu_srt_e_kernel(tc, w, xT, b, offs, out):
         nc.sync.dma_start(w_rows[1][0][:], w_view[1, :, 0, :])
         nc.sync.dma_start(w_rows[1][1][:], w_view[1, :, 1, :])
         nc.sync.dma_start(w_rows[1][2][:], w_view[1, :, 2, :])
-        nc.sync.dma_start(w_rows[1][3][:, 0:1792], w_view[1, :, 3, 0:1792])
+        nc.sync.dma_start(w_rows[1][3][:, 0:1536], w_view[1, :, 3, 0:1536])
+        nc.sync.dma_start(w_rows[1][3][:, 1536:1792], w_view[1, :, 3, 1536:1792])
         nc.sync.dma_start(w_rows[1][3][:, 1792:2048], w_view[1, :, 3, 1792:2048])
         x_codes, x_scales = [None, None], [None, None]
         sums = [psum.tile([P, T], F32, name=f"sums{c}") for c in range(BLOCKS)]
         picked = [keep.tile([P, ROWS, S], F32, name=f"picked{a}") for a in range(PASSES)]
-        slices = [[0, 256], [256, 512], [512, 640], [640, 768]]
-        groups = [[keep.tile([P, s1 - s0, ROWS], BF16, name=f"wg{a}{s0}", align_bytes=64) for (s0, s1) in slices] for a in range(PASSES)]
+        slices = [[[0, 256], [256, 512], [512, 768]], [[0, 128], [128, 256], [256, 384], [384, 512], [512, 640], [640, 768]]]
+        groups = [[keep.tile([P, s1 - s0, ROWS], BF16, name=f"wg{a}{s0}", align_bytes=64) for (s0, s1) in slices[a]] for a in range(PASSES)]
         def do_x(a, eng):
             grouped = keep.tile([P, T, ROWS], BF16, name=f"xg{a}", align_bytes=64)
             eng(grouped[:], x_rows[a][:].rearrange("p j t -> p t j"))
@@ -76,11 +77,11 @@ def tile_picked_neuron_lin_silu_srt_e_kernel(tc, w, xT, b, offs, out):
             )
 
         def weave(a, s, j0, j1, eng):
-            e0, e1 = slices[s]
+            e0, e1 = slices[a][s]
             eng(groups[a][s][:, :, j0:j1], picked[a][:, j0:j1, e0:e1].rearrange("p j n -> p n j"))
 
         def finish(a, s):
-            e0, e1 = slices[s]
+            e0, e1 = slices[a][s]
             codes = keep.tile([P, e1 - e0], U32, name=f"wc{a}{e0}", align_bytes=64)
             scales = keep.tile([P, e1 - e0], U8, name=f"ws{a}{e0}", align_bytes=64)
             nc.vector.quantize_mx(
@@ -89,7 +90,7 @@ def tile_picked_neuron_lin_silu_srt_e_kernel(tc, w, xT, b, offs, out):
             return codes, scales
 
         def multiply(a, s, codes, scales):
-            e0, e1 = slices[s]
+            e0, e1 = slices[a][s]
             for h in range((e1 - e0) // BLOCK):
                 c = e0 // BLOCK + h
                 m = slice(h * BLOCK, (h + 1) * BLOCK)
@@ -104,7 +105,7 @@ def tile_picked_neuron_lin_silu_srt_e_kernel(tc, w, xT, b, offs, out):
                 )
 
         def emit(s):
-            e0, e1 = slices[s]
+            e0, e1 = slices[1][s]
             for c in range(e0 // BLOCK, e1 // BLOCK):
                 result = keep.tile([P, T], F32, name=f"result{c}")
                 nc.scalar.activation(result[:], sums[c][:], SILU, bias=bias[:, c : c + 1])
@@ -127,21 +128,17 @@ def tile_picked_neuron_lin_silu_srt_e_kernel(tc, w, xT, b, offs, out):
         weave(0, 0, 0, 2, Sc)
         weave(0, 1, 0, 2, Sc)
         weave(0, 2, 0, 2, Sc)
-        weave(0, 3, 0, 2, Sc)
         gather(0, 2, 0, S, N)
         gather(0, 3, 0, S, N)
         weave(0, 1, 2, 4, Sc)
         weave(0, 0, 2, 4, V)
         weave(0, 2, 2, 4, V)
-        weave(0, 3, 2, 4, Sc)
         q00 = finish(0, 0)
         q02 = finish(0, 2)
         q01 = finish(0, 1)
-        q03 = finish(0, 3)
         multiply(0, 0, *q00)
         multiply(0, 2, *q02)
         multiply(0, 1, *q01)
-        multiply(0, 3, *q03)
         do_x(1, Sc)
         gather(1, 0, 0, S, N)
         gather(1, 1, 0, S, N)
@@ -149,23 +146,33 @@ def tile_picked_neuron_lin_silu_srt_e_kernel(tc, w, xT, b, offs, out):
         weave(1, 1, 0, 2, Sc)
         weave(1, 2, 0, 2, Sc)
         weave(1, 3, 0, 2, Sc)
+        weave(1, 4, 0, 2, Sc)
+        weave(1, 5, 0, 2, Sc)
         gather(1, 2, 0, S, N)
-        gather(1, 3, 0, 256, 1792)
-        weave(1, 0, 2, 4, Sc)
-        gather(1, 3, 256, 512, 1792)
+        gather(1, 3, 0, 256, 1536)
         weave(1, 1, 2, 4, Sc)
+        weave(1, 0, 2, 4, V)
         q10 = finish(1, 0)
         multiply(1, 0, *q10)
         emit(0)
-        gather(1, 3, 512, 768, N)
-        weave(1, 2, 2, 4, V)
         q11 = finish(1, 1)
         multiply(1, 1, *q11)
         emit(1)
-        weave(1, 3, 2, 4, V)
+        gather(1, 3, 256, 512, 1792)
+        weave(1, 3, 2, 4, Sc)
+        weave(1, 2, 2, 4, V)
         q12 = finish(1, 2)
         multiply(1, 2, *q12)
         emit(2)
         q13 = finish(1, 3)
         multiply(1, 3, *q13)
         emit(3)
+        gather(1, 3, 512, 768, N)
+        weave(1, 5, 2, 4, Sc)
+        weave(1, 4, 2, 4, V)
+        q14 = finish(1, 4)
+        multiply(1, 4, *q14)
+        emit(4)
+        q15 = finish(1, 5)
+        multiply(1, 5, *q15)
+        emit(5)

from contextlib import ExitStack

import concourse.mybir as mybir
from concourse.masks import make_identity

K, T, S, N = 1024, 256, 768, 2048
FLOPS = 2 * K * T * S

F32 = mybir.dt.float32
BF16 = mybir.dt.bfloat16
U32 = mybir.dt.uint32
U16 = mybir.dt.uint16
U8 = mybir.dt.uint8
FP8X4 = mybir.dt.float8_e4m3fn_x4
SILU = mybir.ActivationFunctionType.Silu

P = 128
ROWS = 4
PASSES = K // (P * ROWS)
BLOCK = 128
BLOCKS = S // BLOCK
SLICE = 256
SLICES = S // SLICE


def tile_picked_neuron_lin_silu_srt_e_kernel(tc, w, xT, b, offs, out):
    nc = tc.nc
    with ExitStack() as ctx:
        keep = ctx.enter_context(tc.tile_pool(name="keep", bufs=1))
        psum = ctx.enter_context(tc.psum_pool(name="psum", bufs=1))

        offsets = keep.tile([P, S // 16], U16, name="offsets")
        w_rows = [[keep.tile([P, N], F32, name=f"w{a}{j}") for j in range(ROWS)] for a in range(PASSES)]
        x_rows = [keep.tile([P, ROWS, T], F32, name=f"x{a}") for a in range(PASSES)]

        b_rows = keep.tile([P, P], F32, name="b_rows")
        nc.gpsimd.memset(b_rows[:], 0.0)

        warm = keep.tile([P, 2], F32, name="warm")
        nc.vector.memset(warm[:, 0:1], 0.0)
        nc.scalar.activation(warm[:, 1:2], warm[:, 0:1], SILU)

        w_view = w.rearrange("(a p j) n -> a p j n", a=PASSES, j=ROWS)
        x_view = xT.rearrange("(a p j) t -> a p j t", a=PASSES, j=ROWS)
        nc.sync.dma_start(x_rows[0][:], x_view[0])
        nc.sync.dma_start(offsets[:], offs)
        nc.sync.dma_start(w_rows[0][0][:], w_view[0, :, 0, :])
        nc.sync.dma_start(b_rows[0:BLOCKS, :], b.rearrange("(c p) o -> c (p o)", p=P))
        nc.sync.dma_start(w_rows[0][1][:], w_view[0, :, 1, :])
        nc.sync.dma_start(w_rows[0][2][:], w_view[0, :, 2, :])
        nc.sync.dma_start(w_rows[0][3][:], w_view[0, :, 3, :])
        nc.sync.dma_start(x_rows[1][:], x_view[1])
        nc.sync.dma_start(w_rows[1][0][:], w_view[1, :, 0, :])
        nc.sync.dma_start(w_rows[1][1][:], w_view[1, :, 1, :])
        nc.sync.dma_start(w_rows[1][2][:], w_view[1, :, 2, :])
        nc.sync.dma_start(w_rows[1][3][:, 0:1536], w_view[1, :, 3, 0:1536])
        nc.sync.dma_start(w_rows[1][3][:, 1536:1792], w_view[1, :, 3, 1536:1792])
        nc.sync.dma_start(w_rows[1][3][:, 1792:2048], w_view[1, :, 3, 1792:2048])
        x_codes, x_scales = [None, None], [None, None]
        sums = [psum.tile([P, T], F32, name=f"sums{c}") for c in range(BLOCKS)]
        picked = [keep.tile([P, ROWS, S], F32, name=f"picked{a}") for a in range(PASSES)]
        slices = [[[0, 256], [256, 512], [512, 768]], [[0, 128], [128, 256], [256, 384], [384, 512], [512, 640], [640, 768]]]
        groups = [[keep.tile([P, s1 - s0, ROWS], BF16, name=f"wg{a}{s0}", align_bytes=64) for (s0, s1) in slices[a]] for a in range(PASSES)]
        def do_x(a, eng):
            grouped = keep.tile([P, T, ROWS], BF16, name=f"xg{a}", align_bytes=64)
            eng(grouped[:], x_rows[a][:].rearrange("p j t -> p t j"))
            codes = keep.tile([P, T], U32, name=f"xc{a}", align_bytes=64)
            scales = keep.tile([P, T], U8, name=f"xs{a}", align_bytes=64)
            nc.vector.quantize_mx(
                out=codes[:].bitcast(FP8X4), scales=scales[:], in_=grouped[:].rearrange("p t j -> p (t j)")
            )
            x_codes[a], x_scales[a] = codes, scales

        def gather(a, j, e0, e1, window):
            nc.vector.tensor_copy(
                picked[a][:, j, e0:e1], w_rows[a][j][:, 0:window].indirect(offsets[:, e0 // 16 : e1 // 16])
            )

        def weave(a, s, j0, j1, eng):
            e0, e1 = slices[a][s]
            eng(groups[a][s][:, :, j0:j1], picked[a][:, j0:j1, e0:e1].rearrange("p j n -> p n j"))

        def finish(a, s):
            e0, e1 = slices[a][s]
            codes = keep.tile([P, e1 - e0], U32, name=f"wc{a}{e0}", align_bytes=64)
            scales = keep.tile([P, e1 - e0], U8, name=f"ws{a}{e0}", align_bytes=64)
            nc.vector.quantize_mx(
                out=codes[:].bitcast(FP8X4), scales=scales[:], in_=groups[a][s][:].rearrange("p n j -> p (n j)")
            )
            return codes, scales

        def multiply(a, s, codes, scales):
            e0, e1 = slices[a][s]
            for h in range((e1 - e0) // BLOCK):
                c = e0 // BLOCK + h
                m = slice(h * BLOCK, (h + 1) * BLOCK)
                nc.tensor.matmul_mx(
                    out=sums[c][:],
                    lhsT=codes[:, m].bitcast(FP8X4),
                    lhsT_scale=scales[:, m],
                    rhs=x_codes[a][:].bitcast(FP8X4),
                    rhs_scale=x_scales[a][:],
                    start=(a == 0),
                    stop=(a == 1),
                )

        def emit(s):
            e0, e1 = slices[1][s]
            for c in range(e0 // BLOCK, e1 // BLOCK):
                result = keep.tile([P, T], F32, name=f"result{c}")
                nc.scalar.activation(result[:], sums[c][:], SILU, bias=bias[:, c : c + 1])
                nc.sync.dma_start(out[c * BLOCK : (c + 1) * BLOCK, :], result[:])

        def turn_bias():
            identity = keep.tile([P, P], F32, name="identity")
            bias = keep.tile([P, BLOCKS], F32, name="bias")
            make_identity(nc, identity[:])
            b_turned = psum.tile([P, P], F32, name="b_turned")
            nc.tensor.transpose(b_turned[:], b_rows[:], identity[:])
            nc.scalar.copy(bias[:], b_turned[:, 0:BLOCKS])
            return bias

        V, Sc, G = nc.vector.tensor_copy, nc.scalar.copy, nc.gpsimd.tensor_copy
        do_x(0, V)
        gather(0, 0, 0, S, N)
        gather(0, 1, 0, S, N)
        bias = turn_bias()
        weave(0, 0, 0, 2, Sc)
        weave(0, 1, 0, 2, Sc)
        weave(0, 2, 0, 2, Sc)
        gather(0, 2, 0, S, N)
        gather(0, 3, 0, S, N)
        weave(0, 1, 2, 4, Sc)
        weave(0, 0, 2, 4, V)
        weave(0, 2, 2, 4, V)
        q00 = finish(0, 0)
        q02 = finish(0, 2)
        q01 = finish(0, 1)
        multiply(0, 0, *q00)
        multiply(0, 2, *q02)
        multiply(0, 1, *q01)
        do_x(1, Sc)
        gather(1, 0, 0, S, N)
        gather(1, 1, 0, S, N)
        weave(1, 0, 0, 2, Sc)
        weave(1, 1, 0, 2, Sc)
        weave(1, 2, 0, 2, Sc)
        weave(1, 3, 0, 2, Sc)
        weave(1, 4, 0, 2, Sc)
        weave(1, 5, 0, 2, Sc)
        gather(1, 2, 0, S, N)
        gather(1, 3, 0, 256, 1536)
        weave(1, 1, 2, 4, Sc)
        weave(1, 0, 2, 4, V)
        q10 = finish(1, 0)
        multiply(1, 0, *q10)
        emit(0)
        q11 = finish(1, 1)
        multiply(1, 1, *q11)
        emit(1)
        gather(1, 3, 256, 512, 1792)
        weave(1, 3, 2, 4, Sc)
        weave(1, 2, 2, 4, V)
        q12 = finish(1, 2)
        multiply(1, 2, *q12)
        emit(2)
        q13 = finish(1, 3)
        multiply(1, 3, *q13)
        emit(3)
        gather(1, 3, 512, 768, N)
        weave(1, 5, 2, 4, Sc)
        weave(1, 4, 2, 4, V)
        q14 = finish(1, 4)
        multiply(1, 4, *q14)
        emit(4)
        q15 = finish(1, 5)
        multiply(1, 5, *q15)
        emit(5)
